import numpy as np
import ml_dtypes


def mxq(x, axis, fmt="e4m3"):
    dtype, down = {"e4m3": (ml_dtypes.float8_e4m3fn, 7), "e5m2": (ml_dtypes.float8_e5m2, 14)}[fmt]
    v = np.moveaxis(np.asarray(x, np.float32).astype(ml_dtypes.bfloat16).astype(np.float64), axis, -1)
    blocks = v.reshape(v.shape[:-1] + (-1, 32))
    amax = np.abs(blocks).max(-1, keepdims=True)
    byte = np.maximum(np.where(amax > 0, np.frexp(amax)[1] - 1 + 127, 0) - down, 1)
    scale = np.exp2(byte - 127.0)
    codes = (blocks / scale).astype(np.float32).astype(dtype).astype(np.float64)
    return np.moveaxis((codes * scale).reshape(v.shape), -1, axis)


WIDE = False


def mx_kscale(k):
    if not WIDE:
        return np.ones(k)
    levels = np.array([10, -10, 5, -5, 0])
    if k % 512:
        return np.exp2(np.random.permutation(np.resize(levels, k // 32))).repeat(32)
    a = np.empty((k // 512, 16))
    for p in range(k // 512):
        a[p, :8] = np.random.permutation(np.resize(levels, 8))
        for g in range(8):
            far = levels[np.abs(levels - a[p, g]) >= 10]
            a[p, g + 8] = far[np.random.randint(len(far))]
    return np.exp2(a.ravel()).repeat(32)


def f64(x):
    return np.asarray(x).astype(np.float64)


def striped(idx):
    return np.tile(np.asarray(idx).reshape(-1, 16).T, (8, 1)).astype(np.uint16)


def unstriped(offs):
    return offs[:16].T.reshape(-1).astype(np.int64)


E2M1 = np.array([0.0, 0.5, 1.0, 1.5, 2.0, 3.0, 4.0, 6.0, -0.0, -0.5, -1.0, -1.5, -2.0, -3.0, -4.0, -6.0])


def pack_weight(w, fmt):
    k, n = w.shape
    w = f64(np.asarray(w, np.float32).astype(ml_dtypes.bfloat16)).reshape(k // 32, 32, n)
    amax = np.abs(w).max(1)
    if fmt == "e4m3":
        byte = np.frexp(amax)[1] - 1 + 127 - 7
    else:
        mant, ex = np.frexp(amax / 6.0)
        byte = np.where(mant > 0.5, ex, ex - 1) + 127
    byte = np.clip(np.where(amax > 0, byte, 1), 1, 254)
    scaled = (w * np.exp2(127.0 - byte)[:, None, :]).reshape(k, n).astype(np.float32)
    by_word = np.ascontiguousarray(scaled.reshape(k // 512, 128, 4, n).transpose(0, 1, 3, 2))
    if fmt == "e4m3":
        words = by_word.astype(ml_dtypes.float8_e4m3fn).view(np.uint8)
    else:
        c = by_word.astype(ml_dtypes.float4_e2m1fn).view(np.uint8) & 0xF
        words = (c[..., 0::2] | (c[..., 1::2] << 4)).reshape(k // 512, 128, 2 * n)
    return np.ascontiguousarray(words), np.ascontiguousarray(byte.astype(np.uint8).reshape(k // 512, 16, n))


def unpack_weight(words, scales, fmt):
    g, _, n = scales.shape
    words = np.ascontiguousarray(words).reshape(g, 128, n, -1)
    if fmt == "e4m3":
        vals = words.view(ml_dtypes.float8_e4m3fn).astype(np.float64)
    else:
        nib = np.empty((g, 128, n, 4), np.uint8)
        nib[..., 0::2] = words & 0xF
        nib[..., 1::2] = words >> 4
        vals = E2M1[nib]
    vals = vals * np.repeat(np.exp2(scales.astype(np.float64) - 127.0), 8, axis=1)[..., None]
    return vals.transpose(0, 1, 3, 2).reshape(g * 512, n)


def sgn(shape):
    return np.random.uniform(0.5, 2.0, shape) * np.where(np.random.standard_normal(shape) < 0, -1.0, 1.0)


K, T, J, R, O, U, E = 512, 1024, 256, 512, 128, 128, 256


def setup_inputs():
    n = np.random.standard_normal
    idx = np.random.permutation(T)[:J]
    idx2 = np.random.permutation(J)[:O]
    idx3 = np.random.permutation(J)[:U]
    idx4 = np.random.permutation(E)[:U]
    fk = mx_kscale(K)
    fr = mx_kscale(R)
    xtp = pack_weight(n((K, T)) / fk[:, None], "e2m1")
    wp = pack_weight(n((K, R)) * 1 / np.sqrt(K) * fk[:, None], "e4m3")
    return {
        "xt_words": xtp[0],
        "xt_scales": xtp[1],
        "w_words": wp[0],
        "w_scales": wp[1],
        "sg": (0.35 * sgn((R, 1))).astype(np.float32),
        "lo": (np.random.uniform(-1.0, 1.0, (R, 1)) + np.log(fr)[:, None]).astype(np.float32),
        "sa": (sgn((R, 1)) / fr[:, None] / np.sqrt(R)).astype(np.float32),
        "so": (np.random.uniform(0.5, 1.6, (O, 1))).astype(np.float32),
        "offs": striped(idx),
        "offs2": striped(idx2),
        "offs3": striped(idx3),
        "offs4": striped(idx4),
    }


def reference(xt_words, xt_scales, w_words, w_scales, sg, lo, sa, so, offs, offs2, offs3, offs4):
    idx = unstriped(offs)
    idx2 = unstriped(offs2)
    idx3 = unstriped(offs3)
    idx4 = unstriped(offs4)
    xtu = unpack_weight(xt_words, xt_scales, "e2m1")
    wu = unpack_weight(w_words, w_scales, "e4m3")
    xtidxg = xtu[:, idx]
    a = wu.T @ xtidxg
    z1 = np.exp(a[:, idx2] * f64(sg) + f64(lo))
    z2 = a[:, idx3] * f64(sa)
    z1q = mxq(z1, 0, "e4m3")
    z2q = mxq(z2, 0, "e4m3")
    p = z1q.T @ z2q
    y = np.zeros((O, E))
    y[:, idx4] = p * f64(so)
    return y

from contextlib import ExitStack

import concourse.mybir as mybir

K, T, J, R, O, U, E = 512, 1024, 256, 512, 128, 128, 256
FLOPS = 2 * K * R * J + 2 * R * O * U

F32 = mybir.dt.float32
BF16 = mybir.dt.bfloat16
I32 = mybir.dt.int32
U32 = mybir.dt.uint32
U16 = mybir.dt.uint16
U8 = mybir.dt.uint8
FP8X4 = mybir.dt.float8_e4m3fn_x4
FP4X4 = mybir.dt.float4_e2m1fn_x4
ACT = mybir.ActivationFunctionType

P = 128
PACK = 4
H = U // 2
JH = J // 2


def tile_list_selfenergies_kernel(tc, xt_words, xt_scales, w_words, w_scales, sg, lo, sa, so, offs, offs2, offs3, offs4, out):
    nc = tc.nc
    with ExitStack() as ctx:
        sb = ctx.enter_context(tc.tile_pool(name="sb", bufs=1))
        ps = ctx.enter_context(tc.psum_pool(name="ps", bufs=1))

        idx = sb.tile([P, J // 16], U16, name="idx")
        idx2 = sb.tile([P, O // 16], U16, name="idx2")
        idx3 = sb.tile([P, U // 16], U16, name="idx3")
        idx4 = sb.tile([P, U // 16], U16, name="idx4")
        xw = sb.tile([P, T], U16, name="xw", align_bytes=64)
        xs = sb.tile([P, T], U8, name="xs", align_bytes=64)
        ww = sb.tile([P, R], U32, name="ww", align_bytes=64)
        wst = sb.tile([4, 4, R // 4], I32, name="wst", align_bytes=64)
        ws = sb.tile([P, R], U8, name="ws", align_bytes=64)
        sg_t = sb.tile([P, PACK], F32, name="sg_t", tag="late", align_bytes=64)
        lo_t = sb.tile([P, PACK], F32, name="lo_t")
        sa_t = sb.tile([P, PACK], F32, name="sa_t")
        so_t = sb.tile([P, 1], F32, name="so_t")
        page = sb.tile([P, E], F32, name="page")

        def load_xs(q, eng):
            eng.dma_start(xs[32 * q : 32 * q + 4, :].bitcast(I32), xt_scales[0, 4 * q : 4 * q + 4, :].bitcast(I32))

        nc.vector.memset(xs[:].bitcast(I32), 0)
        warm_in = sb.tile([P, 1], F32, name="warm_in")
        warm_out = sb.tile([P, 1], F32, name="warm_out")
        nc.vector.memset(warm_in[:], 0.0)
        nc.vector.memset(ws[:].bitcast(I32), 0)
        nc.sync.dma_start(wst[:], w_scales[0].bitcast(I32).rearrange("(q r) n -> r q n", r=4))
        nc.sync.dma_start(idx[:], offs)
        nc.sync.dma_start(xw[:].bitcast(I32), xt_words[0].bitcast(I32))
        load_xs(2, nc.scalar)
        load_xs(0, nc.sync)
        load_xs(3, nc.scalar)
        load_xs(1, nc.sync)
        nc.sync.dma_start(ww[:].bitcast(I32), w_words[0].rearrange("p n t -> p (n t)").bitcast(I32))
        nc.scalar.activation(out=warm_out[:], in_=warm_in[:], func=ACT.Exp)

        nc.sync.dma_start(idx2[:], offs2)
        nc.sync.dma_start(sg_t[:], sg.rearrange("(p t) o -> p (t o)", t=PACK))
        nc.sync.dma_start(lo_t[:], lo.rearrange("(p t) o -> p (t o)", t=PACK))
        nc.sync.dma_start(idx3[:], offs3)
        nc.sync.dma_start(sa_t[:], sa.rearrange("(p t) o -> p (t o)", t=PACK))
        nc.sync.dma_start(idx4[:], offs4)
        nc.sync.dma_start(so_t[:], so)
        nc.gpsimd.memset(page[:], 0.0)

        for q in range(4):
            nc.vector.tensor_copy(ws[32 * q : 32 * q + 4, :].bitcast(I32), wst[:, q, :])

        wpw0 = sb.tile([P, P], U32, name="wpw0", align_bytes=64)
        wpw1 = sb.tile([P, PACK - 1, P], U32, name="wpw1", align_bytes=64)
        wpw = [wpw0[:]] + [wpw1[:, t, :] for t in range(PACK - 1)]
        wps0 = sb.tile([P, PACK, P], U8, name="wps0", align_bytes=64)
        nc.gpsimd.tensor_copy(wps0[:], ws[:].rearrange("p (m t) -> p t m", t=PACK))
        wps = [wps0[:, t, :] for t in range(PACK)]
        ww_m = ww[:].rearrange("p (m t) -> p m t", t=PACK)
        nc.scalar.copy(wpw0[:], ww_m[:, :, 0])
        nc.scalar.copy(wpw1[:].rearrange("p t m -> p m t"), ww_m[:, :, 1:])

        xgs = sb.tile([P, J], U8, name="xgs", align_bytes=64)
        xgw = sb.tile([P, J], U16, name="xgw", align_bytes=64)
        a_sb = [sb.tile([P, J], F32, name="a%d" % t) for t in range(PACK)]
        nc.vector.tensor_copy(xgw[:], xw[:].indirect(idx[:]))
        nc.vector.tensor_copy(xgs[:], xs[:].indirect(idx[:]))
        for h in range(2):
            cols = slice(h * JH, (h + 1) * JH)
            acc = ps.tile([P, JH], F32, name="acc0_%d" % h)
            nc.tensor.matmul_mx(acc[:], lhsT=wpw[0].bitcast(FP8X4), lhsT_scale=wps[0],
                                rhs=xgw[:, cols].bitcast(FP4X4), rhs_scale=xgs[:, cols], start=True, stop=True)
            if h == 0:
                nc.scalar.copy(a_sb[0][:, cols], acc[:])
            else:
                nc.vector.tensor_copy(a_sb[0][:, cols], acc[:])
        for t in range(1, PACK):
            acc = ps.tile([P, J], F32, name="acc%d" % t)
            nc.tensor.matmul_mx(acc[:], lhsT=wpw[t].bitcast(FP8X4), lhsT_scale=wps[t],
                                rhs=xgw[:].bitcast(FP4X4), rhs_scale=xgs[:], start=True, stop=True)
            nc.vector.tensor_copy(a_sb[t][:], acc[:])

        z1 = sb.tile([P, PACK * O], BF16, name="z1", align_bytes=64)
        z2 = [sb.tile([P, PACK * H], BF16, name="z2_0", align_bytes=64)]

        def fetch_z2(h, t):
            nc.scalar.activation(out=z2[h][:, t : PACK * H : PACK], in_=a_sb[t][:].indirect(idx3[:, 4 * h : 4 * h + 4]),
                                 func=ACT.Copy, scale=sa_t[:, t : t + 1])

        for t in range(PACK):
            nc.scalar.activation(out=z1[:, t : PACK * O : PACK], in_=a_sb[t][:].indirect(idx2[:]), func=ACT.Exp,
                                 bias=lo_t[:, t : t + 1], scale=sg_t[:, t : t + 1])
            fetch_z2(0, t)
        z1w = sb.tile([P, O], U32, name="z1w", align_bytes=64)
        z1s = sb.tile([P, O], U8, name="z1s", align_bytes=64)
        nc.vector.quantize_mx(z1w[:].bitcast(FP8X4), z1s[:], z1[:])
        z2.append(sb.tile([P, PACK * H], BF16, name="z2_1", tag="late", align_bytes=64))
        for t in range(PACK):
            fetch_z2(1, t)
        for h in range(2):
            z2w = sb.tile([P, H], U32, name="z2w", align_bytes=64)
            z2s = sb.tile([P, H], U8, name="z2s", align_bytes=64)
            nc.vector.quantize_mx(z2w[:].bitcast(FP8X4), z2s[:], z2[h][:])
            pacc = ps.tile([P, H], F32, name="pacc%d" % h)
            nc.tensor.matmul_mx(pacc[:], lhsT=z1w[:].bitcast(FP8X4), lhsT_scale=z1s[:],
                                rhs=z2w[:].bitcast(FP8X4), rhs_scale=z2s[:], start=True, stop=True)
            p_sb = sb.tile([P, H], F32, name="p_sb%d" % h)
            nc.vector.tensor_copy(p_sb[:], pacc[:])
            nc.scalar.activation(out=page[:].indirect(idx4[:, 4 * h : 4 * h + 4]), in_=p_sb[:], func=ACT.Copy, scale=so_t[:])
        nc.sync.dma_start(out, page[:])
